import numpy as np
import ml_dtypes


def mxq(x, axis, fmt="e4m3"):
    dtype, down = {"e4m3": (ml_dtypes.float8_e4m3fn, 7), "e5m2": (ml_dtypes.float8_e5m2, 14)}[fmt]
    v = np.moveaxis(np.asarray(x, np.float32).astype(ml_dtypes.bfloat16).astype(np.float64), axis, -1)
    blocks = v.reshape(v.shape[:-1] + (-1, 32))
    amax = np.abs(blocks).max(-1, keepdims=True)
    byte = np.maximum(np.where(amax > 0, np.frexp(amax)[1] - 1 + 127, 0) - down, 1)
    scale = np.exp2(byte - 127.0)
    codes = (blocks / scale).astype(np.float32).astype(dtype).astype(np.float64)
    return np.moveaxis((codes * scale).reshape(v.shape), -1, axis)


WIDE = False


def mx_kscale(k):
    if not WIDE:
        return np.ones(k)
    levels = np.array([10, -10, 5, -5, 0])
    if k % 512:
        return np.exp2(np.random.permutation(np.resize(levels, k // 32))).repeat(32)
    a = np.empty((k // 512, 16))
    for p in range(k // 512):
        a[p, :8] = np.random.permutation(np.resize(levels, 8))
        for g in range(8):
            far = levels[np.abs(levels - a[p, g]) >= 10]
            a[p, g + 8] = far[np.random.randint(len(far))]
    return np.exp2(a.ravel()).repeat(32)


def f64(x):
    return np.asarray(x).astype(np.float64)


def striped(idx):
    return np.tile(np.asarray(idx).reshape(-1, 16).T, (8, 1)).astype(np.uint16)


def unstriped(offs):
    return offs[:16].T.reshape(-1).astype(np.int64)


def striped8(idx):
    return np.asarray(idx).reshape(8, -1, 16).transpose(0, 2, 1).reshape(128, -1).astype(np.uint16)


def unstriped8(offs):
    return offs.reshape(8, 16, -1).transpose(0, 2, 1).reshape(8, -1).astype(np.int64)


def pick8(x, idx, run):
    r = np.arange(len(x))
    return x[r[:, None], idx[r % (8 * run) // run]]


E2M1 = np.array([0.0, 0.5, 1.0, 1.5, 2.0, 3.0, 4.0, 6.0, -0.0, -0.5, -1.0, -1.5, -2.0, -3.0, -4.0, -6.0])


def pack_weight(w, fmt):
    k, n = w.shape
    w = f64(np.asarray(w, np.float32).astype(ml_dtypes.bfloat16)).reshape(k // 32, 32, n)
    amax = np.abs(w).max(1)
    if fmt == "e4m3":
        byte = np.frexp(amax)[1] - 1 + 127 - 7
    else:
        mant, ex = np.frexp(amax / 6.0)
        byte = np.where(mant > 0.5, ex, ex - 1) + 127
    byte = np.clip(np.where(amax > 0, byte, 1), 1, 254)
    scaled = (w * np.exp2(127.0 - byte)[:, None, :]).reshape(k, n).astype(np.float32)
    by_word = np.ascontiguousarray(scaled.reshape(k // 512, 128, 4, n).transpose(0, 1, 3, 2))
    if fmt == "e4m3":
        words = by_word.astype(ml_dtypes.float8_e4m3fn).view(np.uint8)
    else:
        c = by_word.astype(ml_dtypes.float4_e2m1fn).view(np.uint8) & 0xF
        words = (c[..., 0::2] | (c[..., 1::2] << 4)).reshape(k // 512, 128, 2 * n)
    return np.ascontiguousarray(words), np.ascontiguousarray(byte.astype(np.uint8).reshape(k // 512, 16, n))


def unpack_weight(words, scales, fmt):
    g, _, n = scales.shape
    words = np.ascontiguousarray(words).reshape(g, 128, n, -1)
    if fmt == "e4m3":
        vals = words.view(ml_dtypes.float8_e4m3fn).astype(np.float64)
    else:
        nib = np.empty((g, 128, n, 4), np.uint8)
        nib[..., 0::2] = words & 0xF
        nib[..., 1::2] = words >> 4
        vals = E2M1[nib]
    vals = vals * np.repeat(np.exp2(scales.astype(np.float64) - 127.0), 8, axis=1)[..., None]
    return vals.transpose(0, 1, 3, 2).reshape(g * 512, n)


K, T, J, I, R, N = 512, 1024, 512, 512, 512, 512


def setup_inputs():
    n = np.random.standard_normal
    idx = np.random.permutation(T)[:J]
    idx2 = np.stack([np.random.randint(0, J, I) for _ in range(8)])
    fk = mx_kscale(K)
    fr = mx_kscale(R)
    xtp = pack_weight(n((K, T)) / fk[:, None], "e4m3")
    wap = pack_weight(n((K, R)) * 1 / np.sqrt(K) * fk[:, None] * fr, "e2m1")
    wbp = pack_weight(n((R, N)) * 1 / np.sqrt(R) / fr[:, None], "e4m3")
    return {
        "xt_words": xtp[0],
        "xt_scales": xtp[1],
        "wa_words": wap[0],
        "wa_scales": wap[1],
        "wb_words": wbp[0],
        "wb_scales": wbp[1],
        "rw": (np.random.uniform(0.5, 2.0, (1, I))).astype(np.float32),
        "offs": striped(idx),
        "offs2": striped8(idx2),
    }


def reference(xt_words, xt_scales, wa_words, wa_scales, wb_words, wb_scales, rw, offs, offs2):
    idx = unstriped(offs)
    idx2 = unstriped8(offs2)
    xtu = unpack_weight(xt_words, xt_scales, "e4m3")
    wau = unpack_weight(wa_words, wa_scales, "e2m1")
    wbu = unpack_weight(wb_words, wb_scales, "e4m3")
    xtidxg = xtu[:, idx]
    a = wau.T @ xtidxg
    hid = np.maximum(a, 0.0)
    hididx2q = mxq(pick8(hid, idx2, 64), 0, "e4m3")
    p = wbu.T @ hididx2q
    y = p * f64(rw)
    return y

@@ -1,0 +1,156 @@
+from contextlib import ExitStack
+
+import concourse.mybir as mybir
+
+K, T, J, I, R, N = 512, 1024, 512, 512, 512, 512
+FLOPS = 2 * K * R * J + 2 * R * N * I
+
+F32 = mybir.dt.float32
+BF16 = mybir.dt.bfloat16
+I32 = mybir.dt.int32
+U32 = mybir.dt.uint32
+U16 = mybir.dt.uint16
+U8 = mybir.dt.uint8
+FP8X4 = mybir.dt.float8_e4m3fn_x4
+FP4X4 = mybir.dt.float4_e2m1fn_x4
+RELU = mybir.ActivationFunctionType.Relu
+MULT = mybir.AluOpType.mult
+
+P = 128
+PACK = 4
+PIECE = 128
+PIECES = I // PIECE
+
+
+def load_scale_rows(queue, plane, scales):
+    rows = scales[0].rearrange("(q r) c -> r q c", r=4)
+    for r in range(4):
+        queue.dma_start(out=plane[r:P:32, :].bitcast(I32), in_=rows[r].bitcast(I32))
+
+
+def tile_moe_expert_hidden_slots_swapped_kernel(
+    tc, xt_words, xt_scales, wa_words, wa_scales, wb_words, wb_scales, rw, offs, offs2, out
+):
+    nc = tc.nc
+    with ExitStack() as ctx:
+        keep = ctx.enter_context(tc.tile_pool(name="keep", bufs=1))
+        psum = ctx.enter_context(tc.psum_pool(name="psum", bufs=1))
+
+        token_list = keep.tile([P, J // 16], U16, name="token_list")
+        slot_lists = keep.tile([P, I // 16], U16, name="slot_lists")
+        x_words = keep.tile([P, T], I32, name="x_words", tag="x_words", align_bytes=64)
+        x_plane = keep.tile([P, T], U8, name="x_plane", tag="x_plane", align_bytes=64)
+        wa_raw = keep.tile([P, 2 * R], U8, name="wa_raw", tag="wa_raw", align_bytes=64)
+        wa_raw_plane = keep.tile([P, R], U8, name="wa_raw_plane", tag="wa_raw_plane", align_bytes=64)
+
+        nc.vector.memset(x_plane[:].bitcast(I32), 0)
+        nc.vector.memset(wa_raw_plane[:].bitcast(I32), 0)
+        nc.sync.dma_start(token_list[:], offs)
+        nc.sync.dma_start(slot_lists[:], offs2)
+        load_scale_rows(nc.sync, x_plane, xt_scales)
+        nc.sync.dma_start(out=x_words[:], in_=xt_words[0].rearrange("p c t -> p (c t)").bitcast(I32))
+        nc.sync.dma_start(out=wa_raw[:].bitcast(I32), in_=wa_words[0].bitcast(I32))
+        load_scale_rows(nc.sync, wa_raw_plane, wa_scales)
+
+        xg_plane = keep.tile([P, J], U8, name="xg_plane", align_bytes=64)
+        xg_words = keep.tile([P, J], U32, name="xg_words", align_bytes=64)
+        wa_first = keep.tile([P, 2 * P], U8, name="wa_first", align_bytes=64)
+        wa_plane = keep.tile([P, R], U8, name="wa_plane", align_bytes=64)
+        words_by_t = wa_raw[:].bitcast(U16).rearrange("p (m t) -> p t m", t=PACK)
+        bytes_by_t = wa_raw_plane[:].rearrange("p (m t) -> p t m", t=PACK)
+        nc.vector.tensor_copy(xg_plane[:], x_plane[:].indirect(token_list[:]))
+        nc.vector.tensor_copy(out=wa_first[:].bitcast(U16), in_=words_by_t[:, 0, :])
+        nc.vector.tensor_copy(xg_words[:], x_words[:].bitcast(U32).indirect(token_list[:]))
+        nc.vector.tensor_copy(out=wa_plane[:, 0:P], in_=bytes_by_t[:, 0, :])
+        wa_rest = keep.tile([P, 2 * P * (PACK - 1)], U8, name="wa_rest", tag="x_words", align_bytes=64)
+        nc.vector.tensor_copy(
+            out=wa_rest[:].bitcast(U16).rearrange("p (t m) -> p t m", m=P), in_=words_by_t[:, 1:PACK, :]
+        )
+        nc.vector.tensor_copy(out=wa_plane[:, P:R].rearrange("p (t m) -> p t m", m=P), in_=bytes_by_t[:, 1:PACK, :])
+        wa_cols = [wa_first[:]] + [wa_rest[:, 2 * P * t : 2 * P * (t + 1)] for t in range(PACK - 1)]
+
+        wb = keep.tile([P, N], I32, name="wb", tag="wa_raw", align_bytes=64)
+        wb_plane = keep.tile([P, N], U8, name="wb_plane", tag="wa_raw_plane", align_bytes=64)
+        rw_rows = keep.tile([P, I], F32, name="rw_rows", tag="x_plane", align_bytes=64)
+        nc.sync.dma_start(out=rw_rows[:], in_=rw[0].partition_broadcast(P))
+        nc.sync.dma_start(out=wb[:], in_=wb_words[0].rearrange("p c t -> p (c t)").bitcast(I32))
+        nc.gpsimd.memset(wb_plane[:].bitcast(I32), 0)
+        load_scale_rows(nc.sync, wb_plane, wb_scales)
+
+        half = J // 2
+        hid = [keep.tile([P, J], F32, name="hid%d" % t) for t in range(PACK)]
+        steps = [(0, 0, half), (0, half, J), (1, 0, J), (2, 0, half), (3, 0, half), (2, half, J), (3, half, J)]
+        for s, (t, j0, j1) in enumerate(steps):
+            acc = psum.tile([P, 512], F32, name="acc%d" % s, tag="bank%d" % s)
+            nc.tensor.matmul_mx(
+                out=acc[:, 0 : j1 - j0],
+                lhsT=wa_cols[t].bitcast(FP4X4),
+                lhsT_scale=wa_plane[:, P * t : P * (t + 1)],
+                rhs=xg_words[:, j0:j1].bitcast(FP8X4),
+                rhs_scale=xg_plane[:, j0:j1],
+                start=True,
+                stop=True,
+            )
+            nc.scalar.activation(out=hid[t][:, j0:j1], in_=acc[:, 0 : j1 - j0], func=RELU)
+
+        out_v = out.rearrange("(g p) i -> p g i", p=P)
+        block = PACK * PIECE
+        picked = keep.tile([P, PIECES * block + block // 2], BF16, name="picked", align_bytes=64)
+        woven_at = PIECES * block - block // 2
+        woven = [picked[:, woven_at : woven_at + block]] + [
+            keep.tile([P, block], BF16, name="woven%d" % c, align_bytes=64)[:] for c in range(1, PIECES)
+        ]
+        h_words = [keep.tile([P, PIECE], U32, name="h_words%d" % c, align_bytes=64) for c in range(PIECES)]
+        h_plane = [keep.tile([P, PIECE], U8, name="h_plane%d" % c, align_bytes=64) for c in range(PIECES)]
+
+        def pick(t, c):
+            at = c * block + t * PIECE
+            cols = PIECE // 16
+            nc.vector.tensor_copy(picked[:, at : at + PIECE], hid[t][:].indirect(slot_lists[:, c * cols : (c + 1) * cols]))
+
+        def weave(c):
+            nc.scalar.copy(
+                out=woven[c].rearrange("p (i t) -> p i t", t=PACK),
+                in_=picked[:, c * block : (c + 1) * block].rearrange("p (t i) -> p i t", t=PACK),
+            )
+
+        def quantize(c):
+            nc.vector.quantize_mx(out=h_words[c][:].bitcast(FP8X4), scales=h_plane[c][:], in_=woven[c])
+
+        def second_layer(c, g0, g1, bank):
+            acc = psum.tile([P, g1 - g0, PIECE], F32, name="out_acc%d_%d" % (c, g0), tag="bank%d" % bank)
+            for g in range(g0, g1):
+                nc.tensor.matmul_mx(
+                    out=acc[:, g - g0, :],
+                    lhsT=wb[:, P * g : P * (g + 1)].bitcast(FP8X4),
+                    lhsT_scale=wb_plane[:, P * g : P * (g + 1)],
+                    rhs=h_words[c][:].bitcast(FP8X4),
+                    rhs_scale=h_plane[c][:],
+                    start=True,
+                    stop=True,
+                )
+            places = slice(c * PIECE, (c + 1) * PIECE)
+            res = keep.tile([P, g1 - g0, PIECE], F32, name="res%d_%d" % (c, g0))
+            nc.vector.tensor_tensor(
+                res[:], acc[:], rw_rows[:, places].unsqueeze(1).to_broadcast([P, g1 - g0, PIECE]), MULT
+            )
+            nc.sync.dma_start(out=out_v[:, g0:g1, places], in_=res[:])
+
+        for t in (0, 1):
+            for c in range(PIECES):
+                pick(t, c)
+        for c in range(PIECES - 1):
+            pick(2, c)
+            pick(3, c)
+            weave(c)
+        quantize(0)
+        pick(2, PIECES - 1)
+        pick(3, PIECES - 1)
+        weave(PIECES - 1)
+        for c in range(1, PIECES):
+            quantize(c)
+        second_layer(0, 0, 4, 7)
+        second_layer(1, 0, 4, 0)
+        second_layer(2, 0, 4, 1)
+        second_layer(3, 0, 2, 2)
+        second_layer(3, 2, 4, 3)

@@ -22,10 +22,10 @@ PIECE = 128
 PIECES = I // PIECE
 
 
-def load_scale_rows(queue, plane, scales):
+def load_scale_rows(queues, plane, scales):
     rows = scales[0].rearrange("(q r) c -> r q c", r=4)
     for r in range(4):
-        queue.dma_start(out=plane[r:P:32, :].bitcast(I32), in_=rows[r].bitcast(I32))
+        queues[r].dma_start(out=plane[r:P:32, :].bitcast(I32), in_=rows[r].bitcast(I32))
 
 
 def tile_moe_expert_hidden_slots_swapped_kernel(
@@ -34,11 +34,12 @@ def tile_moe_expert_hidden_slots_swapped_kernel(
     nc = tc.nc
     with ExitStack() as ctx:
         keep = ctx.enter_context(tc.tile_pool(name="keep", bufs=1))
+        reuse = ctx.enter_context(tc.tile_pool(name="reuse", bufs=1))
         psum = ctx.enter_context(tc.psum_pool(name="psum", bufs=1))
 
         token_list = keep.tile([P, J // 16], U16, name="token_list")
         slot_lists = keep.tile([P, I // 16], U16, name="slot_lists")
-        x_words = keep.tile([P, T], I32, name="x_words", tag="x_words", align_bytes=64)
+        x_words = reuse.tile([P, T], I32, name="x_words", offset=0, align_bytes=64)
         x_plane = keep.tile([P, T], U8, name="x_plane", tag="x_plane", align_bytes=64)
         wa_raw = keep.tile([P, 2 * R], U8, name="wa_raw", tag="wa_raw", align_bytes=64)
         wa_raw_plane = keep.tile([P, R], U8, name="wa_raw_plane", tag="wa_raw_plane", align_bytes=64)
@@ -47,45 +48,47 @@ def tile_moe_expert_hidden_slots_swapped_kernel(
         nc.vector.memset(wa_raw_plane[:].bitcast(I32), 0)
         nc.sync.dma_start(token_list[:], offs)
         nc.sync.dma_start(slot_lists[:], offs2)
-        load_scale_rows(nc.sync, x_plane, xt_scales)
-        nc.sync.dma_start(out=x_words[:], in_=xt_words[0].rearrange("p c t -> p (c t)").bitcast(I32))
         nc.sync.dma_start(out=wa_raw[:].bitcast(I32), in_=wa_words[0].bitcast(I32))
-        load_scale_rows(nc.sync, wa_raw_plane, wa_scales)
+        load_scale_rows([nc.sync] * 4, x_plane, xt_scales)
+        nc.sync.dma_start(out=x_words[:], in_=xt_words[0].rearrange("p c t -> p (c t)").bitcast(I32))
+        load_scale_rows([nc.sync] * 4, wa_raw_plane, wa_scales)
 
-        xg_plane = keep.tile([P, J], U8, name="xg_plane", align_bytes=64)
         xg_words = keep.tile([P, J], U32, name="xg_words", align_bytes=64)
-        wa_first = keep.tile([P, 2 * P], U8, name="wa_first", align_bytes=64)
-        wa_plane = keep.tile([P, R], U8, name="wa_plane", align_bytes=64)
+        wa_first = keep.tile([P, 2 * P], U8, name="wa_first", tag="wa_first", align_bytes=64)
+        wa_plane_first = keep.tile([P, P], U8, name="wa_plane_first", align_bytes=64)
         words_by_t = wa_raw[:].bitcast(U16).rearrange("p (m t) -> p t m", t=PACK)
         bytes_by_t = wa_raw_plane[:].rearrange("p (m t) -> p t m", t=PACK)
+        xg_plane = keep.tile([P, J], U8, name="xg_plane", align_bytes=64)
         nc.vector.tensor_copy(xg_plane[:], x_plane[:].indirect(token_list[:]))
         nc.vector.tensor_copy(out=wa_first[:].bitcast(U16), in_=words_by_t[:, 0, :])
         nc.vector.tensor_copy(xg_words[:], x_words[:].bitcast(U32).indirect(token_list[:]))
-        nc.vector.tensor_copy(out=wa_plane[:, 0:P], in_=bytes_by_t[:, 0, :])
-        wa_rest = keep.tile([P, 2 * P * (PACK - 1)], U8, name="wa_rest", tag="x_words", align_bytes=64)
+        nc.vector.tensor_copy(out=wa_plane_first[:], in_=bytes_by_t[:, 0, :])
+        wa_plane_rest = reuse.tile([P, P * (PACK - 1)], U8, name="wa_plane_rest", offset=1024, align_bytes=64)
+        nc.vector.tensor_copy(out=wa_plane_rest[:].rearrange("p (t m) -> p t m", m=P), in_=bytes_by_t[:, 1:PACK, :])
+        wa_rest = reuse.tile([P, 2 * P * (PACK - 1)], U8, name="wa_rest", offset=0, align_bytes=64)
         nc.vector.tensor_copy(
             out=wa_rest[:].bitcast(U16).rearrange("p (t m) -> p t m", m=P), in_=words_by_t[:, 1:PACK, :]
         )
-        nc.vector.tensor_copy(out=wa_plane[:, P:R].rearrange("p (t m) -> p t m", m=P), in_=bytes_by_t[:, 1:PACK, :])
         wa_cols = [wa_first[:]] + [wa_rest[:, 2 * P * t : 2 * P * (t + 1)] for t in range(PACK - 1)]
 
+        wa_planes = [wa_plane_first[:]] + [wa_plane_rest[:, P * t : P * (t + 1)] for t in range(PACK - 1)]
+
         wb = keep.tile([P, N], I32, name="wb", tag="wa_raw", align_bytes=64)
-        wb_plane = keep.tile([P, N], U8, name="wb_plane", tag="wa_raw_plane", align_bytes=64)
-        rw_rows = keep.tile([P, I], F32, name="rw_rows", tag="x_plane", align_bytes=64)
-        nc.sync.dma_start(out=rw_rows[:], in_=rw[0].partition_broadcast(P))
+        wb_plane = keep.tile([P, N], U8, name="wb_plane", tag="x_plane", align_bytes=64)
+        rw_rows = keep.tile([P, I], F32, name="rw_rows", tag="wa_first", align_bytes=64)
         nc.sync.dma_start(out=wb[:], in_=wb_words[0].rearrange("p c t -> p (c t)").bitcast(I32))
         nc.gpsimd.memset(wb_plane[:].bitcast(I32), 0)
-        load_scale_rows(nc.sync, wb_plane, wb_scales)
+        load_scale_rows([nc.sync] * 4, wb_plane, wb_scales)
 
         half = J // 2
         hid = [keep.tile([P, J], F32, name="hid%d" % t) for t in range(PACK)]
-        steps = [(0, 0, half), (0, half, J), (1, 0, J), (2, 0, half), (3, 0, half), (2, half, J), (3, half, J)]
+        steps = [(0, 0, half), (0, half, J), (1, 0, J), (3, 0, J), (2, 0, J)]
         for s, (t, j0, j1) in enumerate(steps):
-            acc = psum.tile([P, 512], F32, name="acc%d" % s, tag="bank%d" % s)
+            acc = psum.tile([P, 512], F32, name="acc%d" % s, tag="bank%d" % (s % 8))
             nc.tensor.matmul_mx(
                 out=acc[:, 0 : j1 - j0],
                 lhsT=wa_cols[t].bitcast(FP4X4),
-                lhsT_scale=wa_plane[:, P * t : P * (t + 1)],
+                lhsT_scale=wa_planes[t],
                 rhs=xg_words[:, j0:j1].bitcast(FP8X4),
                 rhs_scale=xg_plane[:, j0:j1],
                 start=True,
@@ -93,25 +96,27 @@ def tile_moe_expert_hidden_slots_swapped_kernel(
             )
             nc.scalar.activation(out=hid[t][:, j0:j1], in_=acc[:, 0 : j1 - j0], func=RELU)
 
+        nc.sync.dma_start(out=rw_rows[:], in_=rw[0].partition_broadcast(P))
         out_v = out.rearrange("(g p) i -> p g i", p=P)
         block = PACK * PIECE
-        picked = keep.tile([P, PIECES * block + block // 2], BF16, name="picked", align_bytes=64)
-        woven_at = PIECES * block - block // 2
+        picked = keep.tile([P, PACK * I + block // 2], BF16, name="picked", align_bytes=64)
+        woven_at = PACK * I - block // 2
         woven = [picked[:, woven_at : woven_at + block]] + [
             keep.tile([P, block], BF16, name="woven%d" % c, align_bytes=64)[:] for c in range(1, PIECES)
         ]
         h_words = [keep.tile([P, PIECE], U32, name="h_words%d" % c, align_bytes=64) for c in range(PIECES)]
         h_plane = [keep.tile([P, PIECE], U8, name="h_plane%d" % c, align_bytes=64) for c in range(PIECES)]
 
-        def pick(t, c):
-            at = c * block + t * PIECE
-            cols = PIECE // 16
-            nc.vector.tensor_copy(picked[:, at : at + PIECE], hid[t][:].indirect(slot_lists[:, c * cols : (c + 1) * cols]))
+        mid = I // 2
+        planes = picked[:, 0 : PACK * I].rearrange("p (h t i) -> p h t i", h=2, t=PACK)
+
+        def pick(t, i0, i1):
+            nc.vector.tensor_copy(planes[:, i0 // mid, t, i0 % mid : i0 % mid + i1 - i0], hid[t][:].indirect(slot_lists[:, i0 // 16 : i1 // 16]))
 
         def weave(c):
             nc.scalar.copy(
-                out=woven[c].rearrange("p (i t) -> p i t", t=PACK),
-                in_=picked[:, c * block : (c + 1) * block].rearrange("p (t i) -> p i t", t=PACK),
+                out=woven[c].rearrange("p (a b t) -> p a t b", b=4, t=PACK),
+                in_=planes[:, c // 2, :, (c % 2) * PIECE : (c % 2 + 1) * PIECE].rearrange("p t (a b) -> p a t b", b=4),
             )
 
         def quantize(c):
@@ -137,20 +142,21 @@ def tile_moe_expert_hidden_slots_swapped_kernel(
             nc.sync.dma_start(out=out_v[:, g0:g1, places], in_=res[:])
 
         for t in (0, 1):
-            for c in range(PIECES):
-                pick(t, c)
-        for c in range(PIECES - 1):
-            pick(2, c)
-            pick(3, c)
-            weave(c)
+            pick(t, 0, mid)
+            pick(t, mid, I)
+        pick(3, 0, mid)
+        pick(2, 0, mid)
+        weave(0)
+        weave(1)
+        pick(2, mid, I)
         quantize(0)
-        pick(2, PIECES - 1)
-        pick(3, PIECES - 1)
-        weave(PIECES - 1)
+        for c in (2, 3):
+            pick(3, c * PIECE, (c + 1) * PIECE)
+            weave(c)
         for c in range(1, PIECES):
             quantize(c)
-        second_layer(0, 0, 4, 7)
-        second_layer(1, 0, 4, 0)
-        second_layer(2, 0, 4, 1)
-        second_layer(3, 0, 2, 2)
-        second_layer(3, 2, 4, 3)
+        second_layer(0, 0, 4, 5)
+        second_layer(1, 0, 4, 6)
+        second_layer(2, 0, 4, 7)
+        second_layer(3, 0, 2, 0)
+        second_layer(3, 2, 4, 1)

@@ -34,12 +34,11 @@ def tile_moe_expert_hidden_slots_swapped_kernel(
     nc = tc.nc
     with ExitStack() as ctx:
         keep = ctx.enter_context(tc.tile_pool(name="keep", bufs=1))
-        reuse = ctx.enter_context(tc.tile_pool(name="reuse", bufs=1))
         psum = ctx.enter_context(tc.psum_pool(name="psum", bufs=1))
 
         token_list = keep.tile([P, J // 16], U16, name="token_list")
         slot_lists = keep.tile([P, I // 16], U16, name="slot_lists")
-        x_words = reuse.tile([P, T], I32, name="x_words", offset=0, align_bytes=64)
+        x_words = keep.tile([P, T], I32, name="x_words", tag="x_words", align_bytes=64)
         x_plane = keep.tile([P, T], U8, name="x_plane", tag="x_plane", align_bytes=64)
         wa_raw = keep.tile([P, 2 * R], U8, name="wa_raw", tag="wa_raw", align_bytes=64)
         wa_raw_plane = keep.tile([P, R], U8, name="wa_raw_plane", tag="wa_raw_plane", align_bytes=64)
@@ -63,9 +62,9 @@ def tile_moe_expert_hidden_slots_swapped_kernel(
         nc.vector.tensor_copy(out=wa_first[:].bitcast(U16), in_=words_by_t[:, 0, :])
         nc.vector.tensor_copy(xg_words[:], x_words[:].bitcast(U32).indirect(token_list[:]))
         nc.vector.tensor_copy(out=wa_plane_first[:], in_=bytes_by_t[:, 0, :])
-        wa_plane_rest = reuse.tile([P, P * (PACK - 1)], U8, name="wa_plane_rest", offset=1024, align_bytes=64)
+        wa_plane_rest = keep.tile([P, P * (PACK - 1)], U8, name="wa_plane_rest", tag="x_words", align_bytes=64)
         nc.vector.tensor_copy(out=wa_plane_rest[:].rearrange("p (t m) -> p t m", m=P), in_=bytes_by_t[:, 1:PACK, :])
-        wa_rest = reuse.tile([P, 2 * P * (PACK - 1)], U8, name="wa_rest", offset=0, align_bytes=64)
+        wa_rest = keep.tile([P, 2 * P * (PACK - 1)], U8, name="wa_rest", tag="wa_raw_plane", align_bytes=64)
         nc.vector.tensor_copy(
             out=wa_rest[:].bitcast(U16).rearrange("p (t m) -> p t m", m=P), in_=words_by_t[:, 1:PACK, :]
         )
@@ -74,11 +73,10 @@ def tile_moe_expert_hidden_slots_swapped_kernel(
         wa_planes = [wa_plane_first[:]] + [wa_plane_rest[:, P * t : P * (t + 1)] for t in range(PACK - 1)]
 
         wb = keep.tile([P, N], I32, name="wb", tag="wa_raw", align_bytes=64)
-        wb_plane = keep.tile([P, N], U8, name="wb_plane", tag="x_plane", align_bytes=64)
-        rw_rows = keep.tile([P, I], F32, name="rw_rows", tag="wa_first", align_bytes=64)
+        wb_plane = keep.tile([P, N], U8, name="wb_plane", tag="wa_first", align_bytes=64)
+        rw_rows = keep.tile([P, I], F32, name="rw_rows", tag="x_plane", align_bytes=64)
+        nc.sync.dma_start(out=rw_rows[:], in_=rw[0].partition_broadcast(P))
         nc.sync.dma_start(out=wb[:], in_=wb_words[0].rearrange("p c t -> p (c t)").bitcast(I32))
-        nc.gpsimd.memset(wb_plane[:].bitcast(I32), 0)
-        load_scale_rows([nc.sync] * 4, wb_plane, wb_scales)
 
         half = J // 2
         hid = [keep.tile([P, J], F32, name="hid%d" % t) for t in range(PACK)]
@@ -96,13 +94,14 @@ def tile_moe_expert_hidden_slots_swapped_kernel(
             )
             nc.scalar.activation(out=hid[t][:, j0:j1], in_=acc[:, 0 : j1 - j0], func=RELU)
 
-        nc.sync.dma_start(out=rw_rows[:], in_=rw[0].partition_broadcast(P))
+        nc.gpsimd.memset(wb_plane[:].bitcast(I32), 0)
+        load_scale_rows([nc.sync] * 4, wb_plane, wb_scales)
         out_v = out.rearrange("(g p) i -> p g i", p=P)
         block = PACK * PIECE
         picked = keep.tile([P, PACK * I + block // 2], BF16, name="picked", align_bytes=64)
         woven_at = PACK * I - block // 2
         woven = [picked[:, woven_at : woven_at + block]] + [
-            keep.tile([P, block], BF16, name="woven%d" % c, align_bytes=64)[:] for c in range(1, PIECES)
+            keep.tile([P, block], BF16, name="woven%d" % c, tag="woven%d" % c, align_bytes=64)[:] for c in range(1, PIECES)
         ]
         h_words = [keep.tile([P, PIECE], U32, name="h_words%d" % c, align_bytes=64) for c in range(PIECES)]
         h_plane = [keep.tile([P, PIECE], U8, name="h_plane%d" % c, align_bytes=64) for c in range(PIECES)]
@@ -135,7 +134,7 @@ def tile_moe_expert_hidden_slots_swapped_kernel(
                     stop=True,
                 )
             places = slice(c * PIECE, (c + 1) * PIECE)
-            res = keep.tile([P, g1 - g0, PIECE], F32, name="res%d_%d" % (c, g0))
+            res = keep.tile([P, g1 - g0, PIECE], F32, name="res%d_%d" % (c, g0), tag="woven3" if c == 1 else "res%d_%d" % (c, g0), align_bytes=64)
             nc.vector.tensor_tensor(
                 res[:], acc[:], rw_rows[:, places].unsqueeze(1).to_broadcast([P, g1 - g0, PIECE]), MULT
             )

@@ -53,34 +53,30 @@ def tile_moe_expert_hidden_slots_swapped_kernel(
         load_scale_rows([nc.sync] * 4, wa_raw_plane, wa_scales)
 
         xg_words = keep.tile([P, J], U32, name="xg_words", align_bytes=64)
-        wa_first = keep.tile([P, 2 * P], U8, name="wa_first", tag="wa_first", align_bytes=64)
-        wa_plane_first = keep.tile([P, P], U8, name="wa_plane_first", align_bytes=64)
+        wa_perm = keep.tile([P, 2 * R], U8, name="wa_perm", align_bytes=64)
+        wa_plane_first = keep.tile([P, P], U8, name="wa_plane_first", tag="wa_plane_first", align_bytes=64)
         words_by_t = wa_raw[:].bitcast(U16).rearrange("p (m t) -> p t m", t=PACK)
         bytes_by_t = wa_raw_plane[:].rearrange("p (m t) -> p t m", t=PACK)
+        nc.vector.tensor_copy(out=wa_perm[:].bitcast(U16).rearrange("p (t m) -> p t m", m=P), in_=words_by_t)
         xg_plane = keep.tile([P, J], U8, name="xg_plane", align_bytes=64)
         nc.vector.tensor_copy(xg_plane[:], x_plane[:].indirect(token_list[:]))
-        nc.vector.tensor_copy(out=wa_first[:].bitcast(U16), in_=words_by_t[:, 0, :])
         nc.vector.tensor_copy(xg_words[:], x_words[:].bitcast(U32).indirect(token_list[:]))
         nc.vector.tensor_copy(out=wa_plane_first[:], in_=bytes_by_t[:, 0, :])
         wa_plane_rest = keep.tile([P, P * (PACK - 1)], U8, name="wa_plane_rest", tag="x_words", align_bytes=64)
         nc.vector.tensor_copy(out=wa_plane_rest[:].rearrange("p (t m) -> p t m", m=P), in_=bytes_by_t[:, 1:PACK, :])
-        wa_rest = keep.tile([P, 2 * P * (PACK - 1)], U8, name="wa_rest", tag="wa_raw_plane", align_bytes=64)
-        nc.vector.tensor_copy(
-            out=wa_rest[:].bitcast(U16).rearrange("p (t m) -> p t m", m=P), in_=words_by_t[:, 1:PACK, :]
-        )
-        wa_cols = [wa_first[:]] + [wa_rest[:, 2 * P * t : 2 * P * (t + 1)] for t in range(PACK - 1)]
+        wa_cols = [wa_perm[:, 2 * P * t : 2 * P * (t + 1)] for t in range(PACK)]
 
         wa_planes = [wa_plane_first[:]] + [wa_plane_rest[:, P * t : P * (t + 1)] for t in range(PACK - 1)]
 
-        wb = keep.tile([P, N], I32, name="wb", tag="wa_raw", align_bytes=64)
-        wb_plane = keep.tile([P, N], U8, name="wb_plane", tag="wa_first", align_bytes=64)
+        wb = keep.tile([P, N], I32, name="wb", tag="wa_raw_plane", align_bytes=64)
+        wb_plane = keep.tile([P, N], U8, name="wb_plane", tag="wa_plane_first", align_bytes=64)
         rw_rows = keep.tile([P, I], F32, name="rw_rows", tag="x_plane", align_bytes=64)
         nc.sync.dma_start(out=rw_rows[:], in_=rw[0].partition_broadcast(P))
         nc.sync.dma_start(out=wb[:], in_=wb_words[0].rearrange("p c t -> p (c t)").bitcast(I32))
 
         half = J // 2
         hid = [keep.tile([P, J], F32, name="hid%d" % t) for t in range(PACK)]
-        steps = [(0, 0, half), (0, half, J), (1, 0, J), (3, 0, J), (2, 0, J)]
+        steps = [(0, 0, half), (0, half, J), (1, 0, J), (2, 0, J), (3, 0, J)]
         for s, (t, j0, j1) in enumerate(steps):
             acc = psum.tile([P, 512], F32, name="acc%d" % s, tag="bank%d" % (s % 8))
             nc.tensor.matmul_mx(
@@ -98,8 +94,8 @@ def tile_moe_expert_hidden_slots_swapped_kernel(
         load_scale_rows([nc.sync] * 4, wb_plane, wb_scales)
         out_v = out.rearrange("(g p) i -> p g i", p=P)
         block = PACK * PIECE
-        picked = keep.tile([P, PACK * I + block // 2], BF16, name="picked", align_bytes=64)
-        woven_at = PACK * I - block // 2
+        picked = keep.tile([P, PACK * I], BF16, name="picked", align_bytes=64)
+        woven_at = PACK * I - 2 * PIECE - block
         woven = [picked[:, woven_at : woven_at + block]] + [
             keep.tile([P, block], BF16, name="woven%d" % c, tag="woven%d" % c, align_bytes=64)[:] for c in range(1, PIECES)
         ]
@@ -134,26 +130,28 @@ def tile_moe_expert_hidden_slots_swapped_kernel(
                     stop=True,
                 )
             places = slice(c * PIECE, (c + 1) * PIECE)
-            res = keep.tile([P, g1 - g0, PIECE], F32, name="res%d_%d" % (c, g0), tag="woven3" if c == 1 else "res%d_%d" % (c, g0), align_bytes=64)
+            res = keep.tile([P, g1 - g0, PIECE], F32, name="res%d_%d" % (c, g0))
             nc.vector.tensor_tensor(
                 res[:], acc[:], rw_rows[:, places].unsqueeze(1).to_broadcast([P, g1 - g0, PIECE]), MULT
             )
             nc.sync.dma_start(out=out_v[:, g0:g1, places], in_=res[:])
 
-        for t in (0, 1):
-            pick(t, 0, mid)
-            pick(t, mid, I)
-        pick(3, 0, mid)
+        pick(0, 0, mid)
+        pick(0, mid, I)
+        pick(1, 0, mid)
         pick(2, 0, mid)
-        weave(0)
-        weave(1)
-        pick(2, mid, I)
-        quantize(0)
-        for c in (2, 3):
+        for c in (0, 1):
             pick(3, c * PIECE, (c + 1) * PIECE)
             weave(c)
-        for c in range(1, PIECES):
-            quantize(c)
+        pick(3, mid, I)
+        quantize(0)
+        pick(1, mid, I)
+        quantize(1)
+        pick(2, mid, I)
+        weave(2)
+        weave(3)
+        quantize(2)
+        quantize(3)
         second_layer(0, 0, 4, 5)
         second_layer(1, 0, 4, 6)
         second_layer(2, 0, 4, 7)

from contextlib import ExitStack

import concourse.mybir as mybir

K, T, J, I, R, N = 512, 1024, 512, 512, 512, 512
FLOPS = 2 * K * R * J + 2 * R * N * I

F32 = mybir.dt.float32
BF16 = mybir.dt.bfloat16
I32 = mybir.dt.int32
U32 = mybir.dt.uint32
U16 = mybir.dt.uint16
U8 = mybir.dt.uint8
FP8X4 = mybir.dt.float8_e4m3fn_x4
FP4X4 = mybir.dt.float4_e2m1fn_x4
RELU = mybir.ActivationFunctionType.Relu
MULT = mybir.AluOpType.mult

P = 128
PACK = 4
PIECE = 128
PIECES = I // PIECE


def load_scale_rows(queues, plane, scales):
    rows = scales[0].rearrange("(q r) c -> r q c", r=4)
    for r in range(4):
        queues[r].dma_start(out=plane[r:P:32, :].bitcast(I32), in_=rows[r].bitcast(I32))


def tile_moe_expert_hidden_slots_swapped_kernel(
    tc, xt_words, xt_scales, wa_words, wa_scales, wb_words, wb_scales, rw, offs, offs2, out
):
    nc = tc.nc
    with ExitStack() as ctx:
        keep = ctx.enter_context(tc.tile_pool(name="keep", bufs=1))
        psum = ctx.enter_context(tc.psum_pool(name="psum", bufs=1))

        token_list = keep.tile([P, J // 16], U16, name="token_list")
        slot_lists = keep.tile([P, I // 16], U16, name="slot_lists")
        x_words = keep.tile([P, T], I32, name="x_words", tag="x_words", align_bytes=64)
        x_plane = keep.tile([P, T], U8, name="x_plane", tag="x_plane", align_bytes=64)
        wa_raw = keep.tile([P, 2 * R], U8, name="wa_raw", tag="wa_raw", align_bytes=64)
        wa_raw_plane = keep.tile([P, R], U8, name="wa_raw_plane", tag="wa_raw_plane", align_bytes=64)

        nc.vector.memset(x_plane[:].bitcast(I32), 0)
        nc.vector.memset(wa_raw_plane[:].bitcast(I32), 0)
        nc.sync.dma_start(token_list[:], offs)
        nc.sync.dma_start(slot_lists[:], offs2)
        nc.sync.dma_start(out=wa_raw[:].bitcast(I32), in_=wa_words[0].bitcast(I32))
        load_scale_rows([nc.sync] * 4, x_plane, xt_scales)
        nc.sync.dma_start(out=x_words[:], in_=xt_words[0].rearrange("p c t -> p (c t)").bitcast(I32))
        load_scale_rows([nc.sync] * 4, wa_raw_plane, wa_scales)

        xg_words = keep.tile([P, J], U32, name="xg_words", align_bytes=64)
        wa_perm = keep.tile([P, 2 * R], U8, name="wa_perm", align_bytes=64)
        wa_plane_first = keep.tile([P, P], U8, name="wa_plane_first", tag="wa_plane_first", align_bytes=64)
        words_by_t = wa_raw[:].bitcast(U16).rearrange("p (m t) -> p t m", t=PACK)
        bytes_by_t = wa_raw_plane[:].rearrange("p (m t) -> p t m", t=PACK)
        nc.vector.tensor_copy(out=wa_perm[:].bitcast(U16).rearrange("p (t m) -> p t m", m=P), in_=words_by_t)
        xg_plane = keep.tile([P, J], U8, name="xg_plane", align_bytes=64)
        nc.vector.tensor_copy(xg_plane[:], x_plane[:].indirect(token_list[:]))
        nc.vector.tensor_copy(xg_words[:], x_words[:].bitcast(U32).indirect(token_list[:]))
        nc.vector.tensor_copy(out=wa_plane_first[:], in_=bytes_by_t[:, 0, :])
        wa_plane_rest = keep.tile([P, P * (PACK - 1)], U8, name="wa_plane_rest", tag="x_words", align_bytes=64)
        nc.vector.tensor_copy(out=wa_plane_rest[:].rearrange("p (t m) -> p t m", m=P), in_=bytes_by_t[:, 1:PACK, :])
        wa_cols = [wa_perm[:, 2 * P * t : 2 * P * (t + 1)] for t in range(PACK)]

        wa_planes = [wa_plane_first[:]] + [wa_plane_rest[:, P * t : P * (t + 1)] for t in range(PACK - 1)]

        wb = keep.tile([P, N], I32, name="wb", tag="wa_raw_plane", align_bytes=64)
        wb_plane = keep.tile([P, N], U8, name="wb_plane", tag="wa_plane_first", align_bytes=64)
        rw_rows = keep.tile([P, I], F32, name="rw_rows", tag="x_plane", align_bytes=64)
        nc.sync.dma_start(out=rw_rows[:], in_=rw[0].partition_broadcast(P))
        nc.sync.dma_start(out=wb[:], in_=wb_words[0].rearrange("p c t -> p (c t)").bitcast(I32))

        half = J // 2
        hid = [keep.tile([P, J], F32, name="hid%d" % t) for t in range(PACK)]
        steps = [(0, 0, half), (0, half, J), (1, 0, J), (2, 0, J), (3, 0, J)]
        for s, (t, j0, j1) in enumerate(steps):
            acc = psum.tile([P, 512], F32, name="acc%d" % s, tag="bank%d" % (s % 8))
            nc.tensor.matmul_mx(
                out=acc[:, 0 : j1 - j0],
                lhsT=wa_cols[t].bitcast(FP4X4),
                lhsT_scale=wa_planes[t],
                rhs=xg_words[:, j0:j1].bitcast(FP8X4),
                rhs_scale=xg_plane[:, j0:j1],
                start=True,
                stop=True,
            )
            nc.scalar.activation(out=hid[t][:, j0:j1], in_=acc[:, 0 : j1 - j0], func=RELU)

        nc.gpsimd.memset(wb_plane[:].bitcast(I32), 0)
        load_scale_rows([nc.sync] * 4, wb_plane, wb_scales)
        out_v = out.rearrange("(g p) i -> p g i", p=P)
        block = PACK * PIECE
        picked = keep.tile([P, PACK * I], BF16, name="picked", align_bytes=64)
        woven_at = PACK * I - 2 * PIECE - block
        woven = [picked[:, woven_at : woven_at + block]] + [
            keep.tile([P, block], BF16, name="woven%d" % c, tag="woven%d" % c, align_bytes=64)[:] for c in range(1, PIECES)
        ]
        h_words = [keep.tile([P, PIECE], U32, name="h_words%d" % c, align_bytes=64) for c in range(PIECES)]
        h_plane = [keep.tile([P, PIECE], U8, name="h_plane%d" % c, align_bytes=64) for c in range(PIECES)]

        mid = I // 2
        planes = picked[:, 0 : PACK * I].rearrange("p (h t i) -> p h t i", h=2, t=PACK)

        def pick(t, i0, i1):
            nc.vector.tensor_copy(planes[:, i0 // mid, t, i0 % mid : i0 % mid + i1 - i0], hid[t][:].indirect(slot_lists[:, i0 // 16 : i1 // 16]))

        def weave(c):
            nc.scalar.copy(
                out=woven[c].rearrange("p (a b t) -> p a t b", b=4, t=PACK),
                in_=planes[:, c // 2, :, (c % 2) * PIECE : (c % 2 + 1) * PIECE].rearrange("p t (a b) -> p a t b", b=4),
            )

        def quantize(c):
            nc.vector.quantize_mx(out=h_words[c][:].bitcast(FP8X4), scales=h_plane[c][:], in_=woven[c])

        def second_layer(c, g0, g1, bank):
            acc = psum.tile([P, g1 - g0, PIECE], F32, name="out_acc%d_%d" % (c, g0), tag="bank%d" % bank)
            for g in range(g0, g1):
                nc.tensor.matmul_mx(
                    out=acc[:, g - g0, :],
                    lhsT=wb[:, P * g : P * (g + 1)].bitcast(FP8X4),
                    lhsT_scale=wb_plane[:, P * g : P * (g + 1)],
                    rhs=h_words[c][:].bitcast(FP8X4),
                    rhs_scale=h_plane[c][:],
                    start=True,
                    stop=True,
                )
            places = slice(c * PIECE, (c + 1) * PIECE)
            res = keep.tile([P, g1 - g0, PIECE], F32, name="res%d_%d" % (c, g0))
            nc.vector.tensor_tensor(
                res[:], acc[:], rw_rows[:, places].unsqueeze(1).to_broadcast([P, g1 - g0, PIECE]), MULT
            )
            nc.sync.dma_start(out=out_v[:, g0:g1, places], in_=res[:])

        pick(0, 0, mid)
        pick(0, mid, I)
        pick(1, 0, mid)
        pick(2, 0, mid)
        for c in (0, 1):
            pick(3, c * PIECE, (c + 1) * PIECE)
            weave(c)
        pick(3, mid, I)
        quantize(0)
        pick(1, mid, I)
        quantize(1)
        pick(2, mid, I)
        weave(2)
        weave(3)
        quantize(2)
        quantize(3)
        second_layer(0, 0, 4, 5)
        second_layer(1, 0, 4, 6)
        second_layer(2, 0, 4, 7)
        second_layer(3, 0, 2, 0)
        second_layer(3, 2, 4, 1)
